import numpy as np
import ml_dtypes


def mxq(x, axis, fmt="e4m3"):
    dtype, down = {"e4m3": (ml_dtypes.float8_e4m3fn, 7), "e5m2": (ml_dtypes.float8_e5m2, 14)}[fmt]
    v = np.moveaxis(np.asarray(x, np.float32).astype(ml_dtypes.bfloat16).astype(np.float64), axis, -1)
    blocks = v.reshape(v.shape[:-1] + (-1, 32))
    amax = np.abs(blocks).max(-1, keepdims=True)
    byte = np.maximum(np.where(amax > 0, np.frexp(amax)[1] - 1 + 127, 0) - down, 1)
    scale = np.exp2(byte - 127.0)
    codes = (blocks / scale).astype(np.float32).astype(dtype).astype(np.float64)
    return np.moveaxis((codes * scale).reshape(v.shape), -1, axis)


WIDE = False


def mx_kscale(k):
    if not WIDE:
        return np.ones(k)
    levels = np.array([10, -10, 5, -5, 0])
    if k % 512:
        return np.exp2(np.random.permutation(np.resize(levels, k // 32))).repeat(32)
    a = np.empty((k // 512, 16))
    for p in range(k // 512):
        a[p, :8] = np.random.permutation(np.resize(levels, 8))
        for g in range(8):
            far = levels[np.abs(levels - a[p, g]) >= 10]
            a[p, g + 8] = far[np.random.randint(len(far))]
    return np.exp2(a.ravel()).repeat(32)


def f64(x):
    return np.asarray(x).astype(np.float64)


def striped(idx):
    return np.tile(idx.reshape(-1, 16).T, (8, 1)).astype(np.uint16)


def unstriped(offs):
    return offs[:16].T.reshape(-1).astype(np.int64)


def pack_weight(w):
    k, n = w.shape
    w = f64(np.asarray(w, np.float32).astype(ml_dtypes.bfloat16)).reshape(k // 32, 32, n)
    amax = np.abs(w).max(1)
    byte = np.clip(np.where(amax > 0, np.frexp(amax)[1] - 1 + 127 - 7, 1), 1, 254)
    scaled = (w * np.exp2(127.0 - byte)[:, None, :]).reshape(k, n).astype(np.float32)
    words = np.ascontiguousarray(scaled.reshape(k // 512, 128, 4, n).transpose(0, 1, 3, 2)).astype(ml_dtypes.float8_e4m3fn).view(np.uint8)
    return words, np.ascontiguousarray(byte.astype(np.uint8).reshape(k // 512, 16, n))


def unpack_weight(words, scales):
    g, p, n, _ = words.shape
    vals = np.ascontiguousarray(words).view(ml_dtypes.float8_e4m3fn).astype(np.float64) * np.repeat(np.exp2(scales.astype(np.float64) - 127.0), 8, axis=1)[..., None]
    return vals.transpose(0, 1, 3, 2).reshape(g * 512, n)


def sigmoid(v):
    return 1.0 / (1.0 + np.exp(-np.maximum(v, -700.0)))


K, T, S, N = 1024, 2048, 512, 256


def setup_inputs():
    n = np.random.standard_normal
    s = mx_kscale(K)[:, None]
    packed_xT = pack_weight(n((K, T)) * s)
    return {
        "x_words": packed_xT[0],
        "x_scales": packed_xT[1],
        "w1": (n((K, N)) / np.sqrt(K) / s).astype(np.float32),
        "w2": (n((K, N)) / np.sqrt(K) / s).astype(np.float32),
        "offs": striped(np.random.permutation(T)[:S]),
    }


def reference(x_words, x_scales, w1, w2, offs):
    xq = unpack_weight(x_words, x_scales)[:, unstriped(offs)]
    y = mxq(f64(w1), 0, "e4m3").T @ xq
    a = sigmoid(mxq(f64(w2), 0, "e4m3").T @ xq)
    gg = y - (y * a)
    h = gg + a * (np.pad(gg, ((0, 0), (1, 0)))[:, :S])
    rr = a * (np.pad(a, ((0, 0), (1, 0)))[:, :S])
    return h + rr * (np.pad(h, ((0, 0), (2, 0)))[:, :S])

@@ -1,0 +1,151 @@
+from contextlib import ExitStack
+
+import concourse.mybir as mybir
+
+K, T, S, N = 1024, 2048, 512, 256
+FLOPS = 2 * 2 * K * N * S
+
+F32 = mybir.dt.float32
+BF16 = mybir.dt.bfloat16
+I32 = mybir.dt.int32
+U32 = mybir.dt.uint32
+U16 = mybir.dt.uint16
+U8 = mybir.dt.uint8
+FP8X4 = mybir.dt.float8_e4m3fn_x4
+ALU = mybir.AluOpType
+SIGMOID = mybir.ActivationFunctionType.Sigmoid
+
+P = 128
+PACK = 4
+PASSES = K // (P * PACK)
+TILES = N // P
+HALVES = 2
+HALF = S // HALVES
+PAD = 8
+
+
+def tile_picked_yscan_tied_p_kernel(tc, x_words, x_scales, w1, w2, offs, out):
+    nc = tc.nc
+    with ExitStack() as ctx:
+        keep = ctx.enter_context(tc.tile_pool(name="keep", bufs=1))
+        psum = ctx.enter_context(tc.psum_pool(name="psum", bufs=1))
+
+        offsets = keep.tile([P, S // 16], U16, name="offsets")
+        word_table = [keep.tile([P, T], U32, name=f"word_table{o}") for o in range(PASSES)]
+        scale_table = keep.tile([P, T], U8, name="scale_table")
+        words = [keep.tile([P, S], U32, name=f"words{o}", align_bytes=64) for o in range(PASSES)]
+        scales = keep.tile([P, S], U8, name="scales", align_bytes=64)
+
+        gate = [keep.tile([P, PAD + S], F32, name=f"gate{t}") for t in range(TILES)]
+        neg_g = [keep.tile([P, PAD + S], F32, name=f"neg_g{t}") for t in range(TILES)]
+        neg_h = [keep.tile([P, PAD + S], F32, name=f"neg_h{t}") for t in range(TILES)]
+
+        nc.vector.memset(scale_table[:].bitcast(I32), 0)
+        zero = keep.tile([P, PAD], F32, name="zero", tag="staging")
+        nc.vector.memset(zero[:], 0.0)
+        for t in range(TILES):
+            nc.vector.memset(neg_g[t][:, 0:PAD], 0.0)
+            nc.vector.memset(neg_h[t][:, 0:PAD], 0.0)
+
+        for q in range(4):
+            nc.scalar.dma_start(
+                out=scale_table[32 * q : 32 * q + 4 * PASSES, :].bitcast(I32),
+                in_=x_scales[:, 4 * q : 4 * q + 4, :].bitcast(I32),
+            )
+
+        for t in range(TILES):
+            nc.scalar.activation(gate[t][:, 0:PAD], zero[:], SIGMOID)
+        staging = keep.tile([P, 2 * K * N // P], F32, name="staging", tag="staging")
+
+        def load_words(o):
+            nc.sync.dma_start(
+                out=word_table[o][:].bitcast(I32),
+                in_=x_words[o].rearrange("p n r -> p (n r)").bitcast(I32),
+            )
+
+        def load_weight(w, o, c0, c1, at):
+            raw = staging[:, at : at + PACK * (c1 - c0)].rearrange("p (j n) -> p j n", j=PACK)
+            rows = w[o * P * PACK : (o + 1) * P * PACK, c0:c1]
+            nc.sync.dma_start(out=raw, in_=rows.rearrange("(p j) n -> p j n", j=PACK))
+            return raw
+
+        load_words(0)
+        nc.sync.dma_start(offsets[:], offs)
+        load_words(1)
+        raw = {}
+        for o in range(PASSES):
+            whole = load_weight(w2, o, 0, N, o * PACK * N)
+            for t in range(TILES):
+                raw["gate", o, t] = whole[:, :, t * P : (t + 1) * P]
+        for t in range(TILES):
+            for o in range(PASSES):
+                raw["value", o, t] = load_weight(w1, o, t * P, (t + 1) * P, (2 * PASSES + PASSES * t + o) * PACK * P)
+
+        nc.vector.tensor_copy(words[0][:], word_table[0][:].indirect(offsets[:]))
+        nc.vector.tensor_copy(scales[:], scale_table[:].indirect(offsets[:]))
+        nc.vector.tensor_copy(words[1][:], word_table[1][:].indirect(offsets[:]))
+
+        def product(kind, t):
+            banks = [psum.tile([P, HALF], F32, name=f"{kind}_bank{t}{h}") for h in range(HALVES)]
+            for o in range(PASSES):
+                grouped = keep.tile([P, P, PACK], BF16, name=f"{kind}_grouped{o}{t}", align_bytes=64)
+                dst = grouped[:].rearrange("p (c i) j -> p c j i", i=4)
+                src = raw[kind, o, t].rearrange("p j (c i) -> p c j i", i=4)
+                if t == 0:
+                    nc.vector.tensor_copy(out=dst, in_=src)
+                else:
+                    nc.scalar.copy(out=dst, in_=src)
+                codes = keep.tile([P, P], U32, name=f"{kind}_codes{o}{t}", align_bytes=64)
+                plane = keep.tile([P, P], U8, name=f"{kind}_plane{o}{t}", align_bytes=64)
+                nc.vector.quantize_mx(
+                    out=codes[:].bitcast(FP8X4),
+                    scales=plane[:],
+                    in_=grouped[:].rearrange("p c j -> p (c j)"),
+                )
+                for h in range(HALVES):
+                    cols = slice(h * HALF, (h + 1) * HALF)
+                    nc.tensor.matmul_mx(
+                        out=banks[h][:],
+                        lhsT=codes[:].bitcast(FP8X4),
+                        lhsT_scale=plane[:],
+                        rhs=words[o][:, cols].bitcast(FP8X4),
+                        rhs_scale=scales[4 * o : P, cols],
+                        start=(o == 0),
+                        stop=(o == PASSES - 1),
+                    )
+            return banks
+
+        def window(tile, h, back):
+            return tile[:, PAD + h * HALF - back : PAD + (h + 1) * HALF - back]
+
+        rr = []
+        for t in range(TILES):
+            banks = product("gate", t)
+            for h in range(HALVES):
+                nc.scalar.activation(window(gate[t], h, 0), banks[h][:], SIGMOID)
+        for t in range(TILES):
+            pair = keep.tile([P, S], F32, name=f"rr{t}")
+            nc.vector.tensor_tensor(pair[:], gate[t][:, PAD : PAD + S], gate[t][:, PAD - 1 : PAD + S - 1], ALU.mult)
+            rr.append(pair)
+
+        for t in range(TILES):
+            banks = product("value", t)
+            near = keep.tile([P, S], F32, name=f"near{t}")
+            far = keep.tile([P, S], F32, name=f"far{t}")
+            result = keep.tile([P, S], F32, name=f"result{t}")
+            halves = [(h, slice(h * HALF, (h + 1) * HALF)) for h in range(HALVES)]
+            for h, cols in halves:
+                nc.vector.scalar_tensor_tensor(
+                    window(neg_g[t], h, 0), window(gate[t], h, 0), 1.0, banks[h][:], ALU.subtract, ALU.mult
+                )
+            for h, cols in halves:
+                nc.vector.tensor_tensor(near[:, cols], window(gate[t], h, 0), window(neg_g[t], h, 1), ALU.mult)
+            for h, cols in halves:
+                nc.vector.tensor_tensor(window(neg_h[t], h, 0), window(neg_g[t], h, 0), near[:, cols], ALU.add)
+            for h, cols in halves:
+                nc.vector.tensor_tensor(far[:, cols], rr[t][:, cols], window(neg_h[t], h, 2), ALU.mult)
+            for h, cols in halves:
+                nc.vector.scalar_tensor_tensor(
+                    result[:, cols], window(neg_h[t], h, 0), -1.0, far[:, cols], ALU.mult, ALU.subtract
+                )
+                nc.sync.dma_start(out=out[t * P : (t + 1) * P, cols], in_=result[:, cols])

@@ -73,13 +73,11 @@ def tile_picked_yscan_tied_p_kernel(tc, x_words, x_scales, w1, w2, offs, out):
         nc.sync.dma_start(offsets[:], offs)
         load_words(1)
         raw = {}
-        for o in range(PASSES):
-            whole = load_weight(w2, o, 0, N, o * PACK * N)
-            for t in range(TILES):
-                raw["gate", o, t] = whole[:, :, t * P : (t + 1) * P]
-        for t in range(TILES):
+        for m, (kind, w) in enumerate((("gate", w2), ("value", w1))):
             for o in range(PASSES):
-                raw["value", o, t] = load_weight(w1, o, t * P, (t + 1) * P, (2 * PASSES + PASSES * t + o) * PACK * P)
+                rows4 = load_weight(w, o, 0, N, (m * PASSES + o) * PACK * N)
+                for t in range(TILES):
+                    raw[kind, o, t] = rows4[:, :, t * P : (t + 1) * P]
 
         nc.vector.tensor_copy(words[0][:], word_table[0][:].indirect(offsets[:]))
         nc.vector.tensor_copy(scales[:], scale_table[:].indirect(offsets[:]))
@@ -89,8 +87,8 @@ def tile_picked_yscan_tied_p_kernel(tc, x_words, x_scales, w1, w2, offs, out):
             banks = [psum.tile([P, HALF], F32, name=f"{kind}_bank{t}{h}") for h in range(HALVES)]
             for o in range(PASSES):
                 grouped = keep.tile([P, P, PACK], BF16, name=f"{kind}_grouped{o}{t}", align_bytes=64)
-                dst = grouped[:].rearrange("p (c i) j -> p c j i", i=4)
-                src = raw[kind, o, t].rearrange("p j (c i) -> p c j i", i=4)
+                dst = grouped[:]
+                src = raw[kind, o, t].rearrange("p j c -> p c j")
                 if t == 0:
                     nc.vector.tensor_copy(out=dst, in_=src)
                 else:
@@ -128,24 +126,29 @@ def tile_picked_yscan_tied_p_kernel(tc, x_words, x_scales, w1, w2, offs, out):
             nc.vector.tensor_tensor(pair[:], gate[t][:, PAD : PAD + S], gate[t][:, PAD - 1 : PAD + S - 1], ALU.mult)
             rr.append(pair)
 
+        def whole(tile, back):
+            return tile[:, PAD - back : PAD + S - back]
+
+        near = [keep.tile([P, S], F32, name=f"near{t}") for t in range(TILES)]
+        far = [keep.tile([P, S], F32, name=f"far{t}") for t in range(TILES)]
+        result = [keep.tile([P, S], F32, name=f"result{t}") for t in range(TILES)]
+        value_banks = [product("value", t) for t in range(TILES)]
         for t in range(TILES):
-            banks = product("value", t)
-            near = keep.tile([P, S], F32, name=f"near{t}")
-            far = keep.tile([P, S], F32, name=f"far{t}")
-            result = keep.tile([P, S], F32, name=f"result{t}")
-            halves = [(h, slice(h * HALF, (h + 1) * HALF)) for h in range(HALVES)]
-            for h, cols in halves:
+            for h in range(HALVES):
                 nc.vector.scalar_tensor_tensor(
-                    window(neg_g[t], h, 0), window(gate[t], h, 0), 1.0, banks[h][:], ALU.subtract, ALU.mult
+                    window(neg_g[t], h, 0), window(gate[t], h, 0), 1.0, value_banks[t][h][:], ALU.subtract, ALU.mult
                 )
-            for h, cols in halves:
-                nc.vector.tensor_tensor(near[:, cols], window(gate[t], h, 0), window(neg_g[t], h, 1), ALU.mult)
-            for h, cols in halves:
-                nc.vector.tensor_tensor(window(neg_h[t], h, 0), window(neg_g[t], h, 0), near[:, cols], ALU.add)
-            for h, cols in halves:
-                nc.vector.tensor_tensor(far[:, cols], rr[t][:, cols], window(neg_h[t], h, 2), ALU.mult)
-            for h, cols in halves:
+        for t in range(TILES):
+            nc.vector.tensor_tensor(near[t][:], whole(gate[t], 0), whole(neg_g[t], 1), ALU.mult)
+        for t in range(TILES):
+            nc.vector.tensor_tensor(whole(neg_h[t], 0), whole(neg_g[t], 0), near[t][:], ALU.add)
+        for t in range(TILES):
+            nc.vector.tensor_tensor(far[t][:], rr[t][:], whole(neg_h[t], 2), ALU.mult)
+        for t in range(TILES):
+            pieces = t + 1
+            for h in range(pieces):
+                cols = slice(h * S // pieces, (h + 1) * S // pieces)
                 nc.vector.scalar_tensor_tensor(
-                    result[:, cols], window(neg_h[t], h, 0), -1.0, far[:, cols], ALU.mult, ALU.subtract
+                    result[t][:, cols], whole(neg_h[t], 0)[:, cols], -1.0, far[t][:, cols], ALU.mult, ALU.subtract
                 )
-                nc.sync.dma_start(out=out[t * P : (t + 1) * P, cols], in_=result[:, cols])
+                nc.sync.dma_start(out=out[t * P : (t + 1) * P, cols], in_=result[t][:, cols])

@@ -39,23 +39,22 @@ def tile_picked_yscan_tied_p_kernel(tc, x_words, x_scales, w1, w2, offs, out):
         gate = [keep.tile([P, PAD + S], F32, name=f"gate{t}") for t in range(TILES)]
         neg_g = [keep.tile([P, PAD + S], F32, name=f"neg_g{t}") for t in range(TILES)]
         neg_h = [keep.tile([P, PAD + S], F32, name=f"neg_h{t}") for t in range(TILES)]
+        rr = [keep.tile([P, S], F32, name=f"rr{t}") for t in range(TILES)]
+        near = [keep.tile([P, S], F32, name=f"near{t}") for t in range(TILES)]
+        far = [keep.tile([P, S], F32, name=f"far{t}") for t in range(TILES)]
+        result = [keep.tile([P, S], F32, name=f"result{t}") for t in range(TILES)]
+        banks = {
+            (kind, t, h): psum.tile([P, HALF], F32, name=f"{kind}_bank{t}{h}")
+            for kind in ("gate", "value")
+            for t in range(TILES)
+            for h in range(HALVES)
+        }
 
         nc.vector.memset(scale_table[:].bitcast(I32), 0)
-        zero = keep.tile([P, PAD], F32, name="zero", tag="staging")
-        nc.vector.memset(zero[:], 0.0)
         for t in range(TILES):
             nc.vector.memset(neg_g[t][:, 0:PAD], 0.0)
             nc.vector.memset(neg_h[t][:, 0:PAD], 0.0)
-
-        for q in range(4):
-            nc.scalar.dma_start(
-                out=scale_table[32 * q : 32 * q + 4 * PASSES, :].bitcast(I32),
-                in_=x_scales[:, 4 * q : 4 * q + 4, :].bitcast(I32),
-            )
-
-        for t in range(TILES):
-            nc.scalar.activation(gate[t][:, 0:PAD], zero[:], SIGMOID)
-        staging = keep.tile([P, 2 * K * N // P], F32, name="staging", tag="staging")
+            nc.scalar.activation(gate[t][:, 0:PAD], neg_g[t][:, 0:PAD], SIGMOID)
 
         def load_words(o):
             nc.sync.dma_start(
@@ -63,36 +62,35 @@ def tile_picked_yscan_tied_p_kernel(tc, x_words, x_scales, w1, w2, offs, out):
                 in_=x_words[o].rearrange("p n r -> p (n r)").bitcast(I32),
             )
 
-        def load_weight(w, o, c0, c1, at):
-            raw = staging[:, at : at + PACK * (c1 - c0)].rearrange("p (j n) -> p j n", j=PACK)
-            rows = w[o * P * PACK : (o + 1) * P * PACK, c0:c1]
-            nc.sync.dma_start(out=raw, in_=rows.rearrange("(p j) n -> p j n", j=PACK))
+        def load_weight(kind, w, o):
+            raw = keep.tile([P, PACK, N], F32, name=f"{kind}_raw{o}")
+            rows = w[o * P * PACK : (o + 1) * P * PACK, :]
+            nc.sync.dma_start(out=raw[:], in_=rows.rearrange("(p j) n -> p j n", j=PACK))
             return raw
 
         load_words(0)
         nc.sync.dma_start(offsets[:], offs)
+        for q in range(4):
+            nc.sync.dma_start(
+                out=scale_table[32 * q : 32 * q + 4 * PASSES, :].bitcast(I32),
+                in_=x_scales[:, 4 * q : 4 * q + 4, :].bitcast(I32),
+            )
+        gate_raw = [load_weight("gate", w2, o) for o in range(PASSES)]
         load_words(1)
-        raw = {}
-        for m, (kind, w) in enumerate((("gate", w2), ("value", w1))):
-            for o in range(PASSES):
-                rows4 = load_weight(w, o, 0, N, (m * PASSES + o) * PACK * N)
-                for t in range(TILES):
-                    raw[kind, o, t] = rows4[:, :, t * P : (t + 1) * P]
+        value_raw = [load_weight("value", w1, o) for o in range(PASSES)]
 
-        nc.vector.tensor_copy(words[0][:], word_table[0][:].indirect(offsets[:]))
-        nc.vector.tensor_copy(scales[:], scale_table[:].indirect(offsets[:]))
-        nc.vector.tensor_copy(words[1][:], word_table[1][:].indirect(offsets[:]))
+        def half(h):
+            return slice(h * HALF, (h + 1) * HALF)
 
-        def product(kind, t):
-            banks = [psum.tile([P, HALF], F32, name=f"{kind}_bank{t}{h}") for h in range(HALVES)]
-            for o in range(PASSES):
+        def quantise(kind, raw, o):
+            made = []
+            for t in range(TILES):
                 grouped = keep.tile([P, P, PACK], BF16, name=f"{kind}_grouped{o}{t}", align_bytes=64)
-                dst = grouped[:]
-                src = raw[kind, o, t].rearrange("p j c -> p c j")
+                src = raw[:, :, t * P : (t + 1) * P].rearrange("p j c -> p c j")
                 if t == 0:
-                    nc.vector.tensor_copy(out=dst, in_=src)
+                    nc.vector.tensor_copy(out=grouped[:], in_=src)
                 else:
-                    nc.scalar.copy(out=dst, in_=src)
+                    nc.scalar.copy(out=grouped[:], in_=src)
                 codes = keep.tile([P, P], U32, name=f"{kind}_codes{o}{t}", align_bytes=64)
                 plane = keep.tile([P, P], U8, name=f"{kind}_plane{o}{t}", align_bytes=64)
                 nc.vector.quantize_mx(
@@ -100,43 +98,52 @@ def tile_picked_yscan_tied_p_kernel(tc, x_words, x_scales, w1, w2, offs, out):
                     scales=plane[:],
                     in_=grouped[:].rearrange("p c j -> p (c j)"),
                 )
-                for h in range(HALVES):
-                    cols = slice(h * HALF, (h + 1) * HALF)
-                    nc.tensor.matmul_mx(
-                        out=banks[h][:],
-                        lhsT=codes[:].bitcast(FP8X4),
-                        lhsT_scale=plane[:],
-                        rhs=words[o][:, cols].bitcast(FP8X4),
-                        rhs_scale=scales[4 * o : P, cols],
-                        start=(o == 0),
-                        stop=(o == PASSES - 1),
-                    )
-            return banks
+                made.append((codes, plane))
+            return made
+
+        def multiply(kind, weights, o, t, h):
+            codes, plane = weights[t]
+            nc.tensor.matmul_mx(
+                out=banks[kind, t, h][:],
+                lhsT=codes[:].bitcast(FP8X4),
+                lhsT_scale=plane[:],
+                rhs=words[o][:, half(h)].bitcast(FP8X4),
+                rhs_scale=scales[4 * o : P, half(h)],
+                start=(o == 0),
+                stop=(o == PASSES - 1),
+            )
 
         def window(tile, h, back):
             return tile[:, PAD + h * HALF - back : PAD + (h + 1) * HALF - back]
 
-        rr = []
-        for t in range(TILES):
-            banks = product("gate", t)
-            for h in range(HALVES):
-                nc.scalar.activation(window(gate[t], h, 0), banks[h][:], SIGMOID)
-        for t in range(TILES):
-            pair = keep.tile([P, S], F32, name=f"rr{t}")
-            nc.vector.tensor_tensor(pair[:], gate[t][:, PAD : PAD + S], gate[t][:, PAD - 1 : PAD + S - 1], ALU.mult)
-            rr.append(pair)
-
         def whole(tile, back):
             return tile[:, PAD - back : PAD + S - back]
 
-        near = [keep.tile([P, S], F32, name=f"near{t}") for t in range(TILES)]
-        far = [keep.tile([P, S], F32, name=f"far{t}") for t in range(TILES)]
-        result = [keep.tile([P, S], F32, name=f"result{t}") for t in range(TILES)]
-        value_banks = [product("value", t) for t in range(TILES)]
+        nc.vector.tensor_copy(words[0][:], word_table[0][:].indirect(offsets[:]))
+        gate_weights = [quantise("gate", gate_raw[o], o) for o in range(PASSES)]
+        nc.vector.tensor_copy(scales[:], scale_table[:].indirect(offsets[:]))
+        for t in range(TILES):
+            for h in range(HALVES):
+                multiply("gate", gate_weights[0], 0, t, h)
+        for h in range(HALVES):
+            picks = offsets[:, h * HALF // 16 : (h + 1) * HALF // 16]
+            nc.vector.tensor_copy(words[1][:, half(h)], word_table[1][:].indirect(picks))
+            for t in range(TILES):
+                multiply("gate", gate_weights[1], 1, t, h)
+                nc.scalar.activation(window(gate[t], h, 0), banks["gate", t, h][:], SIGMOID)
+
+        for o in range(PASSES):
+            value_weights = quantise("value", value_raw[o], o)
+            for t in range(TILES):
+                for h in range(HALVES):
+                    multiply("value", value_weights, o, t, h)
+        for t in range(TILES):
+            nc.vector.tensor_tensor(rr[t][:], whole(gate[t], 0), whole(gate[t], 1), ALU.mult)
+
         for t in range(TILES):
             for h in range(HALVES):
                 nc.vector.scalar_tensor_tensor(
-                    window(neg_g[t], h, 0), window(gate[t], h, 0), 1.0, value_banks[t][h][:], ALU.subtract, ALU.mult
+                    window(neg_g[t], h, 0), window(gate[t], h, 0), 1.0, banks["value", t, h][:], ALU.subtract, ALU.mult
                 )
         for t in range(TILES):
             nc.vector.tensor_tensor(near[t][:], whole(gate[t], 0), whole(neg_g[t], 1), ALU.mult)

@@ -75,8 +75,9 @@ def tile_picked_yscan_tied_p_kernel(tc, x_words, x_scales, w1, w2, offs, out):
                 out=scale_table[32 * q : 32 * q + 4 * PASSES, :].bitcast(I32),
                 in_=x_scales[:, 4 * q : 4 * q + 4, :].bitcast(I32),
             )
-        gate_raw = [load_weight("gate", w2, o) for o in range(PASSES)]
+        gate_raw = [load_weight("gate", w2, 0)]
         load_words(1)
+        gate_raw.append(load_weight("gate", w2, 1))
         value_raw = [load_weight("value", w1, o) for o in range(PASSES)]
 
         def half(h):
@@ -120,16 +121,15 @@ def tile_picked_yscan_tied_p_kernel(tc, x_words, x_scales, w1, w2, offs, out):
             return tile[:, PAD - back : PAD + S - back]
 
         nc.vector.tensor_copy(words[0][:], word_table[0][:].indirect(offsets[:]))
-        gate_weights = [quantise("gate", gate_raw[o], o) for o in range(PASSES)]
         nc.vector.tensor_copy(scales[:], scale_table[:].indirect(offsets[:]))
+        nc.vector.tensor_copy(words[1][:], word_table[1][:].indirect(offsets[:]))
+        for o in range(PASSES):
+            gate_weights = quantise("gate", gate_raw[o], o)
+            for t in range(TILES):
+                for h in range(HALVES):
+                    multiply("gate", gate_weights, o, t, h)
         for t in range(TILES):
             for h in range(HALVES):
-                multiply("gate", gate_weights[0], 0, t, h)
-        for h in range(HALVES):
-            picks = offsets[:, h * HALF // 16 : (h + 1) * HALF // 16]
-            nc.vector.tensor_copy(words[1][:, half(h)], word_table[1][:].indirect(picks))
-            for t in range(TILES):
-                multiply("gate", gate_weights[1], 1, t, h)
                 nc.scalar.activation(window(gate[t], h, 0), banks["gate", t, h][:], SIGMOID)
 
         for o in range(PASSES):
@@ -138,7 +138,8 @@ def tile_picked_yscan_tied_p_kernel(tc, x_words, x_scales, w1, w2, offs, out):
                 for h in range(HALVES):
                     multiply("value", value_weights, o, t, h)
         for t in range(TILES):
-            nc.vector.tensor_tensor(rr[t][:], whole(gate[t], 0), whole(gate[t], 1), ALU.mult)
+            for h in range(HALVES):
+                nc.vector.tensor_tensor(rr[t][:, half(h)], window(gate[t], h, 0), window(gate[t], h, 1), ALU.mult)
 
         for t in range(TILES):
             for h in range(HALVES):

@@ -62,101 +62,112 @@ def tile_picked_yscan_tied_p_kernel(tc, x_words, x_scales, w1, w2, offs, out):
                 in_=x_words[o].rearrange("p n r -> p (n r)").bitcast(I32),
             )
 
-        def load_weight(kind, w, o):
-            raw = keep.tile([P, PACK, N], F32, name=f"{kind}_raw{o}")
-            rows = w[o * P * PACK : (o + 1) * P * PACK, :]
+        def load_scales():
+            for q in range(4):
+                nc.sync.dma_start(
+                    out=scale_table[32 * q : 32 * q + 4 * PASSES, :].bitcast(I32),
+                    in_=x_scales[:, 4 * q : 4 * q + 4, :].bitcast(I32),
+                )
+
+        def half(h):
+            return slice(h * HALF, (h + 1) * HALF)
+
+        def window(tile, h, back):
+            return tile[:, PAD + h * HALF - back : PAD + (h + 1) * HALF - back]
+
+        def load_weight(kind, o, t):
+            w = w2 if kind == "gate" else w1
+            raw = keep.tile([P, PACK, P], F32, name=f"{kind}_raw{o}{t}")
+            rows = w[o * P * PACK : (o + 1) * P * PACK, t * P : (t + 1) * P]
             nc.sync.dma_start(out=raw[:], in_=rows.rearrange("(p j) n -> p j n", j=PACK))
             return raw
 
         load_words(0)
         nc.sync.dma_start(offsets[:], offs)
-        for q in range(4):
-            nc.sync.dma_start(
-                out=scale_table[32 * q : 32 * q + 4 * PASSES, :].bitcast(I32),
-                in_=x_scales[:, 4 * q : 4 * q + 4, :].bitcast(I32),
-            )
-        gate_raw = [load_weight("gate", w2, 0)]
+        load_scales()
         load_words(1)
-        gate_raw.append(load_weight("gate", w2, 1))
-        value_raw = [load_weight("value", w1, o) for o in range(PASSES)]
+        raw = {
+            (kind, o, t): load_weight(kind, o, t)
+            for t in range(TILES)
+            for kind in ("gate", "value")
+            for o in range(PASSES)
+        }
 
-        def half(h):
-            return slice(h * HALF, (h + 1) * HALF)
+        grouped = {}
+        quantised = {}
 
-        def quantise(kind, raw, o):
-            made = []
-            for t in range(TILES):
-                grouped = keep.tile([P, P, PACK], BF16, name=f"{kind}_grouped{o}{t}", align_bytes=64)
-                src = raw[:, :, t * P : (t + 1) * P].rearrange("p j c -> p c j")
-                if t == 0:
-                    nc.vector.tensor_copy(out=grouped[:], in_=src)
-                else:
-                    nc.scalar.copy(out=grouped[:], in_=src)
-                codes = keep.tile([P, P], U32, name=f"{kind}_codes{o}{t}", align_bytes=64)
-                plane = keep.tile([P, P], U8, name=f"{kind}_plane{o}{t}", align_bytes=64)
-                nc.vector.quantize_mx(
-                    out=codes[:].bitcast(FP8X4),
-                    scales=plane[:],
-                    in_=grouped[:].rearrange("p c j -> p (c j)"),
-                )
-                made.append((codes, plane))
-            return made
+        def cast(kind, o, t, on_vector):
+            tile = keep.tile([P, P, PACK], BF16, name=f"{kind}_grouped{o}{t}", align_bytes=64)
+            src = raw[kind, o, t][:].rearrange("p j c -> p c j")
+            if on_vector:
+                nc.vector.tensor_copy(out=tile[:], in_=src)
+            else:
+                nc.scalar.copy(out=tile[:], in_=src)
+            grouped[kind, o, t] = tile
 
-        def multiply(kind, weights, o, t, h):
-            codes, plane = weights[t]
-            nc.tensor.matmul_mx(
-                out=banks[kind, t, h][:],
-                lhsT=codes[:].bitcast(FP8X4),
-                lhsT_scale=plane[:],
-                rhs=words[o][:, half(h)].bitcast(FP8X4),
-                rhs_scale=scales[4 * o : P, half(h)],
-                start=(o == 0),
-                stop=(o == PASSES - 1),
+        def quantise(kind, o, t):
+            codes = keep.tile([P, P], U32, name=f"{kind}_codes{o}{t}", align_bytes=64)
+            plane = keep.tile([P, P], U8, name=f"{kind}_plane{o}{t}", align_bytes=64)
+            nc.vector.quantize_mx(
+                out=codes[:].bitcast(FP8X4),
+                scales=plane[:],
+                in_=grouped[kind, o, t][:].rearrange("p c j -> p (c j)"),
             )
+            quantised[kind, o, t] = (codes, plane)
 
-        def window(tile, h, back):
-            return tile[:, PAD + h * HALF - back : PAD + (h + 1) * HALF - back]
+        def multiply(kind, o, t):
+            codes, plane = quantised[kind, o, t]
+            for h in range(HALVES):
+                nc.tensor.matmul_mx(
+                    out=banks[kind, t, h][:],
+                    lhsT=codes[:].bitcast(FP8X4),
+                    lhsT_scale=plane[:],
+                    rhs=words[o][:, half(h)].bitcast(FP8X4),
+                    rhs_scale=scales[4 * o : P, half(h)],
+                    start=(o == 0),
+                    stop=(o == PASSES - 1),
+                )
 
-        def whole(tile, back):
-            return tile[:, PAD - back : PAD + S - back]
-
-        nc.vector.tensor_copy(words[0][:], word_table[0][:].indirect(offsets[:]))
-        nc.vector.tensor_copy(scales[:], scale_table[:].indirect(offsets[:]))
-        nc.vector.tensor_copy(words[1][:], word_table[1][:].indirect(offsets[:]))
-        for o in range(PASSES):
-            gate_weights = quantise("gate", gate_raw[o], o)
-            for t in range(TILES):
-                for h in range(HALVES):
-                    multiply("gate", gate_weights, o, t, h)
-        for t in range(TILES):
+        def sigmoid(t):
             for h in range(HALVES):
                 nc.scalar.activation(window(gate[t], h, 0), banks["gate", t, h][:], SIGMOID)
 
-        for o in range(PASSES):
-            value_weights = quantise("value", value_raw[o], o)
-            for t in range(TILES):
-                for h in range(HALVES):
-                    multiply("value", value_weights, o, t, h)
-        for t in range(TILES):
+        def recurrence(t):
             for h in range(HALVES):
                 nc.vector.tensor_tensor(rr[t][:, half(h)], window(gate[t], h, 0), window(gate[t], h, 1), ALU.mult)
-
-        for t in range(TILES):
             for h in range(HALVES):
                 nc.vector.scalar_tensor_tensor(
                     window(neg_g[t], h, 0), window(gate[t], h, 0), 1.0, banks["value", t, h][:], ALU.subtract, ALU.mult
                 )
-        for t in range(TILES):
-            nc.vector.tensor_tensor(near[t][:], whole(gate[t], 0), whole(neg_g[t], 1), ALU.mult)
-        for t in range(TILES):
-            nc.vector.tensor_tensor(whole(neg_h[t], 0), whole(neg_g[t], 0), near[t][:], ALU.add)
-        for t in range(TILES):
-            nc.vector.tensor_tensor(far[t][:], rr[t][:], whole(neg_h[t], 2), ALU.mult)
-        for t in range(TILES):
-            pieces = t + 1
-            for h in range(pieces):
-                cols = slice(h * S // pieces, (h + 1) * S // pieces)
+            for h in range(HALVES):
+                nc.vector.tensor_tensor(near[t][:, half(h)], window(gate[t], h, 0), window(neg_g[t], h, 1), ALU.mult)
+            for h in range(HALVES):
+                nc.vector.tensor_tensor(window(neg_h[t], h, 0), window(neg_g[t], h, 0), near[t][:, half(h)], ALU.add)
+            for h in range(HALVES):
+                nc.vector.tensor_tensor(far[t][:, half(h)], rr[t][:, half(h)], window(neg_h[t], h, 2), ALU.mult)
+            for h in range(HALVES):
                 nc.vector.scalar_tensor_tensor(
-                    result[t][:, cols], whole(neg_h[t], 0)[:, cols], -1.0, far[t][:, cols], ALU.mult, ALU.subtract
+                    result[t][:, half(h)], window(neg_h[t], h, 0), -1.0, far[t][:, half(h)], ALU.mult, ALU.subtract
                 )
-                nc.sync.dma_start(out=out[t * P : (t + 1) * P, cols], in_=result[t][:, cols])
+                nc.sync.dma_start(out=out[t * P : (t + 1) * P, half(h)], in_=result[t][:, half(h)])
+
+        nc.vector.tensor_copy(words[0][:], word_table[0][:].indirect(offsets[:]))
+        nc.vector.tensor_copy(scales[:], scale_table[:].indirect(offsets[:]))
+        nc.vector.tensor_copy(words[1][:], word_table[1][:].indirect(offsets[:]))
+
+        for kind in ("gate", "value"):
+            for o in range(PASSES):
+                cast(kind, o, 0, on_vector=(o == 1))
+        for kind in ("gate", "value"):
+            for o in range(PASSES):
+                quantise(kind, o, 0)
+                multiply(kind, o, 0)
+        sigmoid(0)
+        for kind in ("gate", "value"):
+            for o in range(PASSES):
+                cast(kind, o, 1, on_vector=False)
+                quantise(kind, o, 1)
+                multiply(kind, o, 1)
+        sigmoid(1)
+        for t in range(TILES):
+            recurrence(t)

@@ -62,12 +62,13 @@ def tile_picked_yscan_tied_p_kernel(tc, x_words, x_scales, w1, w2, offs, out):
                 in_=x_words[o].rearrange("p n r -> p (n r)").bitcast(I32),
             )
 
-        def load_scales():
-            for q in range(4):
-                nc.sync.dma_start(
-                    out=scale_table[32 * q : 32 * q + 4 * PASSES, :].bitcast(I32),
-                    in_=x_scales[:, 4 * q : 4 * q + 4, :].bitcast(I32),
-                )
+        def load_scales(rows):
+            for r in rows:
+                for o in range(PASSES):
+                    nc.sync.dma_start(
+                        out=scale_table[4 * o + r : P : 32, :].bitcast(I32),
+                        in_=x_scales[o, r : 16 : 4, :].bitcast(I32),
+                    )
 
         def half(h):
             return slice(h * HALF, (h + 1) * HALF)
@@ -82,16 +83,16 @@ def tile_picked_yscan_tied_p_kernel(tc, x_words, x_scales, w1, w2, offs, out):
             nc.sync.dma_start(out=raw[:], in_=rows.rearrange("(p j) n -> p j n", j=PACK))
             return raw
 
-        load_words(0)
+        pieces = [(kind, o, t) for t in range(TILES) for kind in ("gate", "value") for o in range(PASSES)]
+        raw = {}
         nc.sync.dma_start(offsets[:], offs)
-        load_scales()
+        raw[pieces[0]] = load_weight(*pieces[0])
+        load_scales((0,))
+        load_words(0)
+        load_scales((1, 2, 3))
         load_words(1)
-        raw = {
-            (kind, o, t): load_weight(kind, o, t)
-            for t in range(TILES)
-            for kind in ("gate", "value")
-            for o in range(PASSES)
-        }
+        for piece in pieces[1:]:
+            raw[piece] = load_weight(*piece)
 
         grouped = {}
         quantised = {}
@@ -157,7 +158,7 @@ def tile_picked_yscan_tied_p_kernel(tc, x_words, x_scales, w1, w2, offs, out):
 
         for kind in ("gate", "value"):
             for o in range(PASSES):
-                cast(kind, o, 0, on_vector=(o == 1))
+                cast(kind, o, 0, on_vector=(kind == "value" and o == 1))
         for kind in ("gate", "value"):
             for o in range(PASSES):
                 quantise(kind, o, 0)

@@ -85,8 +85,8 @@ def tile_picked_yscan_tied_p_kernel(tc, x_words, x_scales, w1, w2, offs, out):
 
         pieces = [(kind, o, t) for t in range(TILES) for kind in ("gate", "value") for o in range(PASSES)]
         raw = {}
-        nc.sync.dma_start(offsets[:], offs)
         raw[pieces[0]] = load_weight(*pieces[0])
+        nc.sync.dma_start(offsets[:], offs)
         load_scales((0,))
         load_words(0)
         load_scales((1, 2, 3))
@@ -99,11 +99,12 @@ def tile_picked_yscan_tied_p_kernel(tc, x_words, x_scales, w1, w2, offs, out):
 
         def cast(kind, o, t, on_vector):
             tile = keep.tile([P, P, PACK], BF16, name=f"{kind}_grouped{o}{t}", align_bytes=64)
-            src = raw[kind, o, t][:].rearrange("p j c -> p c j")
+            src = raw[kind, o, t][:].rearrange("p j (c i) -> p c j i", i=4)
+            dst = tile[:].rearrange("p (c i) j -> p c j i", i=4)
             if on_vector:
-                nc.vector.tensor_copy(out=tile[:], in_=src)
+                nc.vector.tensor_copy(out=dst, in_=src)
             else:
-                nc.scalar.copy(out=tile[:], in_=src)
+                nc.scalar.copy(out=dst, in_=src)
             grouped[kind, o, t] = tile
 
         def quantise(kind, o, t):
@@ -133,24 +134,30 @@ def tile_picked_yscan_tied_p_kernel(tc, x_words, x_scales, w1, w2, offs, out):
             for h in range(HALVES):
                 nc.scalar.activation(window(gate[t], h, 0), banks["gate", t, h][:], SIGMOID)
 
-        def recurrence(t):
-            for h in range(HALVES):
-                nc.vector.tensor_tensor(rr[t][:, half(h)], window(gate[t], h, 0), window(gate[t], h, 1), ALU.mult)
-            for h in range(HALVES):
-                nc.vector.scalar_tensor_tensor(
-                    window(neg_g[t], h, 0), window(gate[t], h, 0), 1.0, banks["value", t, h][:], ALU.subtract, ALU.mult
-                )
-            for h in range(HALVES):
-                nc.vector.tensor_tensor(near[t][:, half(h)], window(gate[t], h, 0), window(neg_g[t], h, 1), ALU.mult)
-            for h in range(HALVES):
-                nc.vector.tensor_tensor(window(neg_h[t], h, 0), window(neg_g[t], h, 0), near[t][:, half(h)], ALU.add)
-            for h in range(HALVES):
-                nc.vector.tensor_tensor(far[t][:, half(h)], rr[t][:, half(h)], window(neg_h[t], h, 2), ALU.mult)
-            for h in range(HALVES):
-                nc.vector.scalar_tensor_tensor(
-                    result[t][:, half(h)], window(neg_h[t], h, 0), -1.0, far[t][:, half(h)], ALU.mult, ALU.subtract
-                )
-                nc.sync.dma_start(out=out[t * P : (t + 1) * P, half(h)], in_=result[t][:, half(h)])
+        def pair_gates(t, h):
+            nc.vector.tensor_tensor(rr[t][:, half(h)], window(gate[t], h, 0), window(gate[t], h, 1), ALU.mult)
+
+        def gated_input(t, h):
+            nc.vector.scalar_tensor_tensor(
+                window(neg_g[t], h, 0), window(gate[t], h, 0), 1.0, banks["value", t, h][:], ALU.subtract, ALU.mult
+            )
+
+        def near_term(t, h):
+            nc.vector.tensor_tensor(near[t][:, half(h)], window(gate[t], h, 0), window(neg_g[t], h, 1), ALU.mult)
+
+        def first_round(t, h):
+            nc.vector.tensor_tensor(window(neg_h[t], h, 0), window(neg_g[t], h, 0), near[t][:, half(h)], ALU.add)
+
+        def far_term(t, h):
+            nc.vector.tensor_tensor(far[t][:, half(h)], rr[t][:, half(h)], window(neg_h[t], h, 2), ALU.mult)
+
+        def second_round(t, h):
+            nc.vector.scalar_tensor_tensor(
+                result[t][:, half(h)], window(neg_h[t], h, 0), -1.0, far[t][:, half(h)], ALU.mult, ALU.subtract
+            )
+            nc.sync.dma_start(out=out[t * P : (t + 1) * P, half(h)], in_=result[t][:, half(h)])
+
+        steps = (pair_gates, gated_input, near_term, first_round, far_term, second_round)
 
         nc.vector.tensor_copy(words[0][:], word_table[0][:].indirect(offsets[:]))
         nc.vector.tensor_copy(scales[:], scale_table[:].indirect(offsets[:]))
@@ -164,11 +171,20 @@ def tile_picked_yscan_tied_p_kernel(tc, x_words, x_scales, w1, w2, offs, out):
                 quantise(kind, o, 0)
                 multiply(kind, o, 0)
         sigmoid(0)
-        for kind in ("gate", "value"):
-            for o in range(PASSES):
-                cast(kind, o, 1, on_vector=False)
-                quantise(kind, o, 1)
-                multiply(kind, o, 1)
-        sigmoid(1)
-        for t in range(TILES):
-            recurrence(t)
+        later = pieces[2 * PASSES :]
+        for piece in later:
+            cast(*piece, on_vector=False)
+        placed = 0
+        for n, step in enumerate(steps):
+            for h in range(HALVES):
+                step(0, h)
+                if (n, h) in ((2, 1), (3, 1), (4, 1), (5, 0)):
+                    piece = later[placed]
+                    placed = placed + 1
+                    quantise(*piece)
+                    multiply(*piece)
+                    if piece == ("gate", PASSES - 1, 1):
+                        sigmoid(1)
+        for step in steps:
+            for h in range(HALVES):
+                step(1, h)

@@ -86,12 +86,13 @@ def tile_picked_yscan_tied_p_kernel(tc, x_words, x_scales, w1, w2, offs, out):
         pieces = [(kind, o, t) for t in range(TILES) for kind in ("gate", "value") for o in range(PASSES)]
         raw = {}
         raw[pieces[0]] = load_weight(*pieces[0])
+        raw[pieces[1]] = load_weight(*pieces[1])
         nc.sync.dma_start(offsets[:], offs)
         load_scales((0,))
         load_words(0)
         load_scales((1, 2, 3))
         load_words(1)
-        for piece in pieces[1:]:
+        for piece in pieces[2:]:
             raw[piece] = load_weight(*piece)
 
         grouped = {}
@@ -152,16 +153,22 @@ def tile_picked_yscan_tied_p_kernel(tc, x_words, x_scales, w1, w2, offs, out):
             nc.vector.tensor_tensor(far[t][:, half(h)], rr[t][:, half(h)], window(neg_h[t], h, 2), ALU.mult)
 
         def second_round(t, h):
-            nc.vector.scalar_tensor_tensor(
-                result[t][:, half(h)], window(neg_h[t], h, 0), -1.0, far[t][:, half(h)], ALU.mult, ALU.subtract
-            )
-            nc.sync.dma_start(out=out[t * P : (t + 1) * P, half(h)], in_=result[t][:, half(h)])
+            pieces_out = 2 if (t, h) == (TILES - 1, HALVES - 1) else 1
+            width = HALF // pieces_out
+            for n in range(pieces_out):
+                cols = slice(h * HALF + n * width, h * HALF + (n + 1) * width)
+                nc.vector.scalar_tensor_tensor(
+                    result[t][:, cols], neg_h[t][:, PAD : PAD + S][:, cols], -1.0, far[t][:, cols], ALU.mult, ALU.subtract
+                )
+                nc.sync.dma_start(out=out[t * P : (t + 1) * P, cols], in_=result[t][:, cols])
 
         steps = (pair_gates, gated_input, near_term, first_round, far_term, second_round)
 
         nc.vector.tensor_copy(words[0][:], word_table[0][:].indirect(offsets[:]))
         nc.vector.tensor_copy(scales[:], scale_table[:].indirect(offsets[:]))
-        nc.vector.tensor_copy(words[1][:], word_table[1][:].indirect(offsets[:]))
+        for h in range(HALVES):
+            part = offsets[:, h * HALF // 16 : (h + 1) * HALF // 16]
+            nc.vector.tensor_copy(words[1][:, half(h)], word_table[1][:].indirect(part))
 
         for kind in ("gate", "value"):
             for o in range(PASSES):

@@ -62,13 +62,13 @@ def tile_picked_yscan_tied_p_kernel(tc, x_words, x_scales, w1, w2, offs, out):
                 in_=x_words[o].rearrange("p n r -> p (n r)").bitcast(I32),
             )
 
-        def load_scales(rows):
-            for r in rows:
-                for o in range(PASSES):
-                    nc.sync.dma_start(
-                        out=scale_table[4 * o + r : P : 32, :].bitcast(I32),
-                        in_=x_scales[o, r : 16 : 4, :].bitcast(I32),
-                    )
+        def load_scales(first, last):
+            for n in range(first, last):
+                r, o = divmod(n, PASSES)
+                nc.sync.dma_start(
+                    out=scale_table[4 * o + r : P : 32, :].bitcast(I32),
+                    in_=x_scales[o, r : 16 : 4, :].bitcast(I32),
+                )
 
         def half(h):
             return slice(h * HALF, (h + 1) * HALF)
@@ -85,12 +85,12 @@ def tile_picked_yscan_tied_p_kernel(tc, x_words, x_scales, w1, w2, offs, out):
 
         pieces = [(kind, o, t) for t in range(TILES) for kind in ("gate", "value") for o in range(PASSES)]
         raw = {}
-        raw[pieces[0]] = load_weight(*pieces[0])
-        raw[pieces[1]] = load_weight(*pieces[1])
-        nc.sync.dma_start(offsets[:], offs)
-        load_scales((0,))
+        for piece in pieces[:2]:
+            raw[piece] = load_weight(*piece)
+        load_scales(0, 5)
         load_words(0)
-        load_scales((1, 2, 3))
+        nc.sync.dma_start(offsets[:], offs)
+        load_scales(5, 8)
         load_words(1)
         for piece in pieces[2:]:
             raw[piece] = load_weight(*piece)

@@ -1,6 +1,7 @@
 from contextlib import ExitStack
 
 import concourse.mybir as mybir
+from concourse.masks import make_identity
 
 K, T, S, N = 1024, 2048, 512, 256
 FLOPS = 2 * 2 * K * N * S
@@ -14,6 +15,7 @@ U8 = mybir.dt.uint8
 FP8X4 = mybir.dt.float8_e4m3fn_x4
 ALU = mybir.AluOpType
 SIGMOID = mybir.ActivationFunctionType.Sigmoid
+COPY = mybir.ActivationFunctionType.Copy
 
 P = 128
 PACK = 4
@@ -50,7 +52,10 @@ def tile_picked_yscan_tied_p_kernel(tc, x_words, x_scales, w1, w2, offs, out):
             for h in range(HALVES)
         }
 
+        identity = keep.tile([P, P], F32, name="identity")
         nc.vector.memset(scale_table[:].bitcast(I32), 0)
+        nc.vector.memset(identity[:], 0.0)
+        make_identity(nc, identity[:], nomemset=True)
         for t in range(TILES):
             nc.vector.memset(neg_g[t][:, 0:PAD], 0.0)
             nc.vector.memset(neg_h[t][:, 0:PAD], 0.0)
@@ -78,19 +83,23 @@ def tile_picked_yscan_tied_p_kernel(tc, x_words, x_scales, w1, w2, offs, out):
 
         def load_weight(kind, o, t):
             w = w2 if kind == "gate" else w1
-            raw = keep.tile([P, PACK, P], F32, name=f"{kind}_raw{o}{t}")
+            if (kind, o, t) == ("value", 1, 0):
+                flat = rr[0][:]
+            else:
+                flat = keep.tile([P, PACK * P], F32, name=f"{kind}_raw{o}{t}")[:]
+            raw = flat.rearrange("p (j n) -> p j n", j=PACK)
             rows = w[o * P * PACK : (o + 1) * P * PACK, t * P : (t + 1) * P]
-            nc.sync.dma_start(out=raw[:], in_=rows.rearrange("(p j) n -> p j n", j=PACK))
+            nc.sync.dma_start(out=raw, in_=rows.rearrange("(p j) n -> p j n", j=PACK))
             return raw
 
         pieces = [(kind, o, t) for t in range(TILES) for kind in ("gate", "value") for o in range(PASSES)]
         raw = {}
         for piece in pieces[:2]:
             raw[piece] = load_weight(*piece)
-        load_scales(0, 5)
-        load_words(0)
         nc.sync.dma_start(offsets[:], offs)
-        load_scales(5, 8)
+        load_scales(0, 2)
+        load_words(0)
+        load_scales(2, 8)
         load_words(1)
         for piece in pieces[2:]:
             raw[piece] = load_weight(*piece)
@@ -100,7 +109,7 @@ def tile_picked_yscan_tied_p_kernel(tc, x_words, x_scales, w1, w2, offs, out):
 
         def cast(kind, o, t, on_vector):
             tile = keep.tile([P, P, PACK], BF16, name=f"{kind}_grouped{o}{t}", align_bytes=64)
-            src = raw[kind, o, t][:].rearrange("p j (c i) -> p c j i", i=4)
+            src = raw[kind, o, t].rearrange("p j (c i) -> p c j i", i=4)
             dst = tile[:].rearrange("p (c i) j -> p c j i", i=4)
             if on_vector:
                 nc.vector.tensor_copy(out=dst, in_=src)
@@ -143,6 +152,7 @@ def tile_picked_yscan_tied_p_kernel(tc, x_words, x_scales, w1, w2, offs, out):
                 window(neg_g[t], h, 0), window(gate[t], h, 0), 1.0, banks["value", t, h][:], ALU.subtract, ALU.mult
             )
 
+
         def near_term(t, h):
             nc.vector.tensor_tensor(near[t][:, half(h)], window(gate[t], h, 0), window(neg_g[t], h, 1), ALU.mult)
 
@@ -162,6 +172,21 @@ def tile_picked_yscan_tied_p_kernel(tc, x_words, x_scales, w1, w2, offs, out):
                 )
                 nc.sync.dma_start(out=out[t * P : (t + 1) * P, cols], in_=result[t][:, cols])
 
+        def second_round_turned(t, h):
+            turned_bank = psum.tile([P, HALF], F32, name=f"gate_bank{t}{h}")
+            for b in range(HALF // P):
+                cols = slice(h * HALF + b * P, h * HALF + (b + 1) * P)
+                block = turned_bank[:, b * P : (b + 1) * P]
+                nc.tensor.matmul(block, neg_h[t][:, PAD : PAD + S][:, cols], identity[:], start=True, stop=False, is_transpose=True)
+                nc.tensor.matmul(block, far[t][:, cols], identity[:], start=False, stop=True, is_transpose=True)
+            turned = keep.tile([P, HALF], F32, name=f"turned{h}")
+            nc.scalar.activation(turned[:], turned_bank[:], COPY, scale=-1.0)
+            back_bank = psum.tile([P, HALF], F32, name=f"value_bank{t}{h}")
+            for b in range(HALF // P):
+                nc.tensor.transpose(back_bank[:, b * P : (b + 1) * P], turned[:, b * P : (b + 1) * P], identity[:])
+            nc.scalar.copy(out=result[t][:, half(h)], in_=back_bank[:])
+            nc.sync.dma_start(out=out[t * P : (t + 1) * P, half(h)], in_=result[t][:, half(h)])
+
         steps = (pair_gates, gated_input, near_term, first_round, far_term, second_round)
 
         nc.vector.tensor_copy(words[0][:], word_table[0][:].indirect(offsets[:]))
@@ -170,28 +195,28 @@ def tile_picked_yscan_tied_p_kernel(tc, x_words, x_scales, w1, w2, offs, out):
             part = offsets[:, h * HALF // 16 : (h + 1) * HALF // 16]
             nc.vector.tensor_copy(words[1][:, half(h)], word_table[1][:].indirect(part))
 
-        for kind in ("gate", "value"):
-            for o in range(PASSES):
-                cast(kind, o, 0, on_vector=(kind == "value" and o == 1))
-        for kind in ("gate", "value"):
-            for o in range(PASSES):
-                quantise(kind, o, 0)
-                multiply(kind, o, 0)
+        for kind, o, t in pieces[: 2 * PASSES]:
+            cast(kind, o, t, on_vector=(kind == "value" and o == 1))
+        for piece in pieces[: 2 * PASSES]:
+            quantise(*piece)
+            multiply(*piece)
         sigmoid(0)
         later = pieces[2 * PASSES :]
         for piece in later:
             cast(*piece, on_vector=False)
         placed = 0
-        for n, step in enumerate(steps):
+        for n, step in enumerate(steps[:-1]):
             for h in range(HALVES):
                 step(0, h)
-                if (n, h) in ((2, 1), (3, 1), (4, 1), (5, 0)):
+                if (n, h) in ((1, 1), (2, 1), (3, 1), (4, 1)):
                     piece = later[placed]
                     placed = placed + 1
                     quantise(*piece)
                     multiply(*piece)
                     if piece == ("gate", PASSES - 1, 1):
                         sigmoid(1)
+        for h in range(HALVES):
+            second_round_turned(0, h)
         for step in steps:
             for h in range(HALVES):
                 step(1, h)

@@ -96,10 +96,10 @@ def tile_picked_yscan_tied_p_kernel(tc, x_words, x_scales, w1, w2, offs, out):
         raw = {}
         for piece in pieces[:2]:
             raw[piece] = load_weight(*piece)
-        nc.sync.dma_start(offsets[:], offs)
-        load_scales(0, 2)
+        load_scales(0, 5)
         load_words(0)
-        load_scales(2, 8)
+        nc.sync.dma_start(offsets[:], offs)
+        load_scales(5, 8)
         load_words(1)
         for piece in pieces[2:]:
             raw[piece] = load_weight(*piece)
@@ -215,8 +215,8 @@ def tile_picked_yscan_tied_p_kernel(tc, x_words, x_scales, w1, w2, offs, out):
                     multiply(*piece)
                     if piece == ("gate", PASSES - 1, 1):
                         sigmoid(1)
-        for h in range(HALVES):
-            second_round_turned(0, h)
+        second_round(0, 1)
+        second_round_turned(0, 0)
         for step in steps:
             for h in range(HALVES):
                 step(1, h)

@@ -45,6 +45,8 @@ def tile_picked_yscan_tied_p_kernel(tc, x_words, x_scales, w1, w2, offs, out):
         near = [keep.tile([P, S], F32, name=f"near{t}") for t in range(TILES)]
         far = [keep.tile([P, S], F32, name=f"far{t}") for t in range(TILES)]
         result = [keep.tile([P, S], F32, name=f"result{t}") for t in range(TILES)]
+        warm_bank = psum.tile([P, S], F32, name="value_bank11")
+        planes = keep.tile([P, 2 * PASSES * P], U8, name="planes", align_bytes=64)
         banks = {
             (kind, t, h): psum.tile([P, HALF], F32, name=f"{kind}_bank{t}{h}")
             for kind in ("gate", "value")
@@ -55,6 +57,7 @@ def tile_picked_yscan_tied_p_kernel(tc, x_words, x_scales, w1, w2, offs, out):
         identity = keep.tile([P, P], F32, name="identity")
         nc.vector.memset(scale_table[:].bitcast(I32), 0)
         nc.vector.memset(identity[:], 0.0)
+        nc.vector.memset(planes[:].bitcast(I32), 0)
         make_identity(nc, identity[:], nomemset=True)
         for t in range(TILES):
             nc.vector.memset(neg_g[t][:, 0:PAD], 0.0)
@@ -119,10 +122,14 @@ def tile_picked_yscan_tied_p_kernel(tc, x_words, x_scales, w1, w2, offs, out):
 
         def quantise(kind, o, t):
             codes = keep.tile([P, P], U32, name=f"{kind}_codes{o}{t}", align_bytes=64)
-            plane = keep.tile([P, P], U8, name=f"{kind}_plane{o}{t}", align_bytes=64)
+            if t == 0:
+                n = pieces.index((kind, o, t))
+                plane = planes[:, n * P : (n + 1) * P]
+            else:
+                plane = keep.tile([P, P], U8, name=f"{kind}_plane{o}{t}", align_bytes=64)[:]
             nc.vector.quantize_mx(
                 out=codes[:].bitcast(FP8X4),
-                scales=plane[:],
+                scales=plane,
                 in_=grouped[kind, o, t][:].rearrange("p c j -> p (c j)"),
             )
             quantised[kind, o, t] = (codes, plane)
@@ -133,7 +140,7 @@ def tile_picked_yscan_tied_p_kernel(tc, x_words, x_scales, w1, w2, offs, out):
                 nc.tensor.matmul_mx(
                     out=banks[kind, t, h][:],
                     lhsT=codes[:].bitcast(FP8X4),
-                    lhsT_scale=plane[:],
+                    lhsT_scale=plane,
                     rhs=words[o][:, half(h)].bitcast(FP8X4),
                     rhs_scale=scales[4 * o : P, half(h)],
                     start=(o == 0),
@@ -197,7 +204,22 @@ def tile_picked_yscan_tied_p_kernel(tc, x_words, x_scales, w1, w2, offs, out):
 
         for kind, o, t in pieces[: 2 * PASSES]:
             cast(kind, o, t, on_vector=(kind == "value" and o == 1))
-        for piece in pieces[: 2 * PASSES]:
+        for piece in pieces[:PASSES]:
+            quantise(*piece)
+        for piece in pieces[:PASSES]:
+            codes, plane = quantised[piece]
+            nc.tensor.matmul_mx(
+                out=warm_bank[:],
+                lhsT=codes[:].bitcast(FP8X4),
+                lhsT_scale=plane,
+                rhs=words[0][:].bitcast(FP8X4),
+                rhs_scale=planes[:],
+                start=True,
+                stop=True,
+            )
+        for piece in pieces[:PASSES]:
+            multiply(*piece)
+        for piece in pieces[PASSES : 2 * PASSES]:
             quantise(*piece)
             multiply(*piece)
         sigmoid(0)

@@ -43,7 +43,7 @@ def tile_picked_yscan_tied_p_kernel(tc, x_words, x_scales, w1, w2, offs, out):
         neg_h = [keep.tile([P, PAD + S], F32, name=f"neg_h{t}") for t in range(TILES)]
         rr = [keep.tile([P, S], F32, name=f"rr{t}") for t in range(TILES)]
         near = [keep.tile([P, S], F32, name=f"near{t}") for t in range(TILES)]
-        far = [keep.tile([P, S], F32, name=f"far{t}") for t in range(TILES)]
+        far = [keep.tile([P, S], F32, name=f"far{t}", align_bytes=64) for t in range(TILES)]
         result = [keep.tile([P, S], F32, name=f"result{t}") for t in range(TILES)]
         warm_bank = psum.tile([P, S], F32, name="value_bank11")
         planes = keep.tile([P, 2 * PASSES * P], U8, name="planes", align_bytes=64)
@@ -111,9 +111,12 @@ def tile_picked_yscan_tied_p_kernel(tc, x_words, x_scales, w1, w2, offs, out):
         quantised = {}
 
         def cast(kind, o, t, on_vector):
-            tile = keep.tile([P, P, PACK], BF16, name=f"{kind}_grouped{o}{t}", align_bytes=64)
+            if (kind, o, t) == ("value", 1, 1):
+                tile = far[0][:, half(1)].bitcast(BF16)
+            else:
+                tile = keep.tile([P, P * PACK], BF16, name=f"{kind}_grouped{o}{t}", align_bytes=64)[:]
             src = raw[kind, o, t].rearrange("p j (c i) -> p c j i", i=4)
-            dst = tile[:].rearrange("p (c i) j -> p c j i", i=4)
+            dst = tile.rearrange("p (c i j) -> p c j i", i=4, j=PACK)
             if on_vector:
                 nc.vector.tensor_copy(out=dst, in_=src)
             else:
@@ -130,7 +133,7 @@ def tile_picked_yscan_tied_p_kernel(tc, x_words, x_scales, w1, w2, offs, out):
             nc.vector.quantize_mx(
                 out=codes[:].bitcast(FP8X4),
                 scales=plane,
-                in_=grouped[kind, o, t][:].rearrange("p c j -> p (c j)"),
+                in_=grouped[kind, o, t],
             )
             quantised[kind, o, t] = (codes, plane)
 
@@ -179,20 +182,32 @@ def tile_picked_yscan_tied_p_kernel(tc, x_words, x_scales, w1, w2, offs, out):
                 )
                 nc.sync.dma_start(out=out[t * P : (t + 1) * P, cols], in_=result[t][:, cols])
 
-        def second_round_turned(t, h):
-            turned_bank = psum.tile([P, HALF], F32, name=f"gate_bank{t}{h}")
+        turned_banks = {}
+
+        def turn_term(term, t, h, first):
+            if first:
+                turned_banks[h] = psum.tile([P, HALF], F32, name=f"gate_bank{t}{h}")
             for b in range(HALF // P):
                 cols = slice(h * HALF + b * P, h * HALF + (b + 1) * P)
-                block = turned_bank[:, b * P : (b + 1) * P]
-                nc.tensor.matmul(block, neg_h[t][:, PAD : PAD + S][:, cols], identity[:], start=True, stop=False, is_transpose=True)
-                nc.tensor.matmul(block, far[t][:, cols], identity[:], start=False, stop=True, is_transpose=True)
+                nc.tensor.matmul(
+                    turned_banks[h][:, b * P : (b + 1) * P],
+                    term[:, cols],
+                    identity[:],
+                    start=(first and b == 0),
+                    stop=(not first and b == HALF // P - 1),
+                    is_transpose=True,
+                )
+
+        def second_round_turned(t, h):
+            turned_bank = turned_banks[h]
+            turn_term(far[t][:], t, h, False)
             turned = keep.tile([P, HALF], F32, name=f"turned{h}")
             nc.scalar.activation(turned[:], turned_bank[:], COPY, scale=-1.0)
             back_bank = psum.tile([P, HALF], F32, name=f"value_bank{t}{h}")
             for b in range(HALF // P):
                 nc.tensor.transpose(back_bank[:, b * P : (b + 1) * P], turned[:, b * P : (b + 1) * P], identity[:])
             nc.scalar.copy(out=result[t][:, half(h)], in_=back_bank[:])
-            nc.sync.dma_start(out=out[t * P : (t + 1) * P, half(h)], in_=result[t][:, half(h)])
+            nc.scalar.dma_start(out=out[t * P : (t + 1) * P, half(h)], in_=result[t][:, half(h)])
 
         steps = (pair_gates, gated_input, near_term, first_round, far_term, second_round)
 
@@ -230,15 +245,17 @@ def tile_picked_yscan_tied_p_kernel(tc, x_words, x_scales, w1, w2, offs, out):
         for n, step in enumerate(steps[:-1]):
             for h in range(HALVES):
                 step(0, h)
-                if (n, h) in ((1, 1), (2, 1), (3, 1), (4, 1)):
+                if step is first_round:
+                    turn_term(neg_h[0][:, PAD : PAD + S], 0, h, True)
+                if (n, h) in ((1, 1), (2, 1), (3, 1), (4, 0)):
                     piece = later[placed]
                     placed = placed + 1
                     quantise(*piece)
                     multiply(*piece)
                     if piece == ("gate", PASSES - 1, 1):
                         sigmoid(1)
-        second_round(0, 1)
-        second_round_turned(0, 0)
+        for h in range(HALVES):
+            second_round_turned(0, h)
         for step in steps:
             for h in range(HALVES):
                 step(1, h)

@@ -108,6 +108,7 @@ def tile_picked_yscan_tied_p_kernel(tc, x_words, x_scales, w1, w2, offs, out):
             raw[piece] = load_weight(*piece)
 
         grouped = {}
+        shared = []
         quantised = {}
 
         def cast(kind, o, t, on_vector):
@@ -119,6 +120,9 @@ def tile_picked_yscan_tied_p_kernel(tc, x_words, x_scales, w1, w2, offs, out):
             dst = tile.rearrange("p (c i j) -> p c j i", i=4, j=PACK)
             if on_vector:
                 nc.vector.tensor_copy(out=dst, in_=src)
+            elif (kind, o, t) == pieces[-1]:
+                nc.scalar.copy(out=dst[:, :16], in_=src[:, :16])
+                shared.append((dst[:, 16:], src[:, 16:]))
             else:
                 nc.scalar.copy(out=dst, in_=src)
             grouped[kind, o, t] = tile
@@ -245,6 +249,8 @@ def tile_picked_yscan_tied_p_kernel(tc, x_words, x_scales, w1, w2, offs, out):
         for n, step in enumerate(steps[:-1]):
             for h in range(HALVES):
                 step(0, h)
+                if (n, h) == (3, 0):
+                    nc.vector.tensor_copy(out=shared[0][0], in_=shared[0][1])
                 if step is first_round:
                     turn_term(neg_h[0][:, PAD : PAD + S], 0, h, True)
                 if (n, h) in ((1, 1), (2, 1), (3, 1), (4, 0)):

@@ -45,8 +45,6 @@ def tile_picked_yscan_tied_p_kernel(tc, x_words, x_scales, w1, w2, offs, out):
         near = [keep.tile([P, S], F32, name=f"near{t}") for t in range(TILES)]
         far = [keep.tile([P, S], F32, name=f"far{t}", align_bytes=64) for t in range(TILES)]
         result = [keep.tile([P, S], F32, name=f"result{t}") for t in range(TILES)]
-        warm_bank = psum.tile([P, S], F32, name="value_bank11")
-        planes = keep.tile([P, 2 * PASSES * P], U8, name="planes", align_bytes=64)
         banks = {
             (kind, t, h): psum.tile([P, HALF], F32, name=f"{kind}_bank{t}{h}")
             for kind in ("gate", "value")
@@ -57,7 +55,6 @@ def tile_picked_yscan_tied_p_kernel(tc, x_words, x_scales, w1, w2, offs, out):
         identity = keep.tile([P, P], F32, name="identity")
         nc.vector.memset(scale_table[:].bitcast(I32), 0)
         nc.vector.memset(identity[:], 0.0)
-        nc.vector.memset(planes[:].bitcast(I32), 0)
         make_identity(nc, identity[:], nomemset=True)
         for t in range(TILES):
             nc.vector.memset(neg_g[t][:, 0:PAD], 0.0)
@@ -129,11 +126,7 @@ def tile_picked_yscan_tied_p_kernel(tc, x_words, x_scales, w1, w2, offs, out):
 
         def quantise(kind, o, t):
             codes = keep.tile([P, P], U32, name=f"{kind}_codes{o}{t}", align_bytes=64)
-            if t == 0:
-                n = pieces.index((kind, o, t))
-                plane = planes[:, n * P : (n + 1) * P]
-            else:
-                plane = keep.tile([P, P], U8, name=f"{kind}_plane{o}{t}", align_bytes=64)[:]
+            plane = keep.tile([P, P], U8, name=f"{kind}_plane{o}{t}", align_bytes=64)[:]
             nc.vector.quantize_mx(
                 out=codes[:].bitcast(FP8X4),
                 scales=plane,
@@ -141,9 +134,9 @@ def tile_picked_yscan_tied_p_kernel(tc, x_words, x_scales, w1, w2, offs, out):
             )
             quantised[kind, o, t] = (codes, plane)
 
-        def multiply(kind, o, t):
+        def multiply(kind, o, t, halves=range(HALVES)):
             codes, plane = quantised[kind, o, t]
-            for h in range(HALVES):
+            for h in halves:
                 nc.tensor.matmul_mx(
                     out=banks[kind, t, h][:],
                     lhsT=codes[:].bitcast(FP8X4),
@@ -226,21 +219,12 @@ def tile_picked_yscan_tied_p_kernel(tc, x_words, x_scales, w1, w2, offs, out):
         for piece in pieces[:PASSES]:
             quantise(*piece)
         for piece in pieces[:PASSES]:
-            codes, plane = quantised[piece]
-            nc.tensor.matmul_mx(
-                out=warm_bank[:],
-                lhsT=codes[:].bitcast(FP8X4),
-                lhsT_scale=plane,
-                rhs=words[0][:].bitcast(FP8X4),
-                rhs_scale=planes[:],
-                start=True,
-                stop=True,
-            )
-        for piece in pieces[:PASSES]:
             multiply(*piece)
         for piece in pieces[PASSES : 2 * PASSES]:
             quantise(*piece)
-            multiply(*piece)
+        for h in range(HALVES):
+            for piece in pieces[PASSES : 2 * PASSES]:
+                multiply(*piece, [h])
         sigmoid(0)
         later = pieces[2 * PASSES :]
         for piece in later:

@@ -34,7 +34,7 @@ def tile_picked_yscan_tied_p_kernel(tc, x_words, x_scales, w1, w2, offs, out):
 
         offsets = keep.tile([P, S // 16], U16, name="offsets")
         word_table = [keep.tile([P, T], U32, name=f"word_table{o}") for o in range(PASSES)]
-        scale_table = keep.tile([P, T], U8, name="scale_table")
+        scale_table = keep.tile([P, T], U8, name="scale_table", tag="scale_table", align_bytes=64)
         words = [keep.tile([P, S], U32, name=f"words{o}", align_bytes=64) for o in range(PASSES)]
         scales = keep.tile([P, S], U8, name="scales", align_bytes=64)
 
@@ -45,6 +45,9 @@ def tile_picked_yscan_tied_p_kernel(tc, x_words, x_scales, w1, w2, offs, out):
         near = [keep.tile([P, S], F32, name=f"near{t}") for t in range(TILES)]
         far = [keep.tile([P, S], F32, name=f"far{t}", align_bytes=64) for t in range(TILES)]
         result = [keep.tile([P, S], F32, name=f"result{t}") for t in range(TILES)]
+        warm_bank = psum.tile([P, S], F32, name="value_bank11")
+        first_codes = keep.tile([P, PASSES * P], U32, name="first_codes", align_bytes=64)
+        first_planes = keep.tile([P, PASSES * P], U8, name="first_planes", align_bytes=64)
         banks = {
             (kind, t, h): psum.tile([P, HALF], F32, name=f"{kind}_bank{t}{h}")
             for kind in ("gate", "value")
@@ -125,10 +128,14 @@ def tile_picked_yscan_tied_p_kernel(tc, x_words, x_scales, w1, w2, offs, out):
             grouped[kind, o, t] = tile
 
         def quantise(kind, o, t):
-            codes = keep.tile([P, P], U32, name=f"{kind}_codes{o}{t}", align_bytes=64)
-            plane = keep.tile([P, P], U8, name=f"{kind}_plane{o}{t}", align_bytes=64)[:]
+            if (kind, t) == ("gate", 0):
+                codes = first_codes[:, o * P : (o + 1) * P]
+                plane = first_planes[:, o * P : (o + 1) * P]
+            else:
+                codes = keep.tile([P, P], U32, name=f"{kind}_codes{o}{t}", align_bytes=64)[:]
+                plane = keep.tile([P, P], U8, name=f"{kind}_plane{o}{t}", align_bytes=64)[:]
             nc.vector.quantize_mx(
-                out=codes[:].bitcast(FP8X4),
+                out=codes.bitcast(FP8X4),
                 scales=plane,
                 in_=grouped[kind, o, t],
             )
@@ -139,7 +146,7 @@ def tile_picked_yscan_tied_p_kernel(tc, x_words, x_scales, w1, w2, offs, out):
             for h in halves:
                 nc.tensor.matmul_mx(
                     out=banks[kind, t, h][:],
-                    lhsT=codes[:].bitcast(FP8X4),
+                    lhsT=codes.bitcast(FP8X4),
                     lhsT_scale=plane,
                     rhs=words[o][:, half(h)].bitcast(FP8X4),
                     rhs_scale=scales[4 * o : P, half(h)],
@@ -218,6 +225,18 @@ def tile_picked_yscan_tied_p_kernel(tc, x_words, x_scales, w1, w2, offs, out):
             cast(kind, o, t, on_vector=(kind == "value" and o == 1))
         for piece in pieces[:PASSES]:
             quantise(*piece)
+        warm_codes = keep.tile([P, P], U32, name="warm_codes", tag="scale_table", align_bytes=64)
+        nc.scalar.copy(out=warm_codes[:], in_=first_codes[:, 0:P])
+        for start, width in ((0, 2 * P), (2 * P, P)):
+            nc.tensor.matmul_mx(
+                out=warm_bank[:, start : start + width],
+                lhsT=warm_codes[:].bitcast(FP8X4),
+                lhsT_scale=first_planes[:, 0:P],
+                rhs=first_codes[:, 0:width].bitcast(FP8X4),
+                rhs_scale=first_planes[:, 0:width],
+                start=True,
+                stop=True,
+            )
         for piece in pieces[:PASSES]:
             multiply(*piece)
         for piece in pieces[PASSES : 2 * PASSES]:

from contextlib import ExitStack

import concourse.mybir as mybir
from concourse.masks import make_identity

K, T, S, N = 1024, 2048, 512, 256
FLOPS = 2 * 2 * K * N * S

F32 = mybir.dt.float32
BF16 = mybir.dt.bfloat16
I32 = mybir.dt.int32
U32 = mybir.dt.uint32
U16 = mybir.dt.uint16
U8 = mybir.dt.uint8
FP8X4 = mybir.dt.float8_e4m3fn_x4
ALU = mybir.AluOpType
SIGMOID = mybir.ActivationFunctionType.Sigmoid
COPY = mybir.ActivationFunctionType.Copy

P = 128
PACK = 4
PASSES = K // (P * PACK)
TILES = N // P
HALVES = 2
HALF = S // HALVES
PAD = 8


def tile_picked_yscan_tied_p_kernel(tc, x_words, x_scales, w1, w2, offs, out):
    nc = tc.nc
    with ExitStack() as ctx:
        keep = ctx.enter_context(tc.tile_pool(name="keep", bufs=1))
        psum = ctx.enter_context(tc.psum_pool(name="psum", bufs=1))

        offsets = keep.tile([P, S // 16], U16, name="offsets")
        word_table = [keep.tile([P, T], U32, name=f"word_table{o}") for o in range(PASSES)]
        scale_table = keep.tile([P, T], U8, name="scale_table", tag="scale_table", align_bytes=64)
        words = [keep.tile([P, S], U32, name=f"words{o}", align_bytes=64) for o in range(PASSES)]
        scales = keep.tile([P, S], U8, name="scales", align_bytes=64)

        gate = [keep.tile([P, PAD + S], F32, name=f"gate{t}") for t in range(TILES)]
        neg_g = [keep.tile([P, PAD + S], F32, name=f"neg_g{t}") for t in range(TILES)]
        neg_h = [keep.tile([P, PAD + S], F32, name=f"neg_h{t}") for t in range(TILES)]
        rr = [keep.tile([P, S], F32, name=f"rr{t}") for t in range(TILES)]
        near = [keep.tile([P, S], F32, name=f"near{t}") for t in range(TILES)]
        far = [keep.tile([P, S], F32, name=f"far{t}", align_bytes=64) for t in range(TILES)]
        result = [keep.tile([P, S], F32, name=f"result{t}") for t in range(TILES)]
        warm_bank = psum.tile([P, S], F32, name="value_bank11")
        first_codes = keep.tile([P, PASSES * P], U32, name="first_codes", align_bytes=64)
        first_planes = keep.tile([P, PASSES * P], U8, name="first_planes", align_bytes=64)
        banks = {
            (kind, t, h): psum.tile([P, HALF], F32, name=f"{kind}_bank{t}{h}")
            for kind in ("gate", "value")
            for t in range(TILES)
            for h in range(HALVES)
        }

        identity = keep.tile([P, P], F32, name="identity")
        nc.vector.memset(scale_table[:].bitcast(I32), 0)
        nc.vector.memset(identity[:], 0.0)
        make_identity(nc, identity[:], nomemset=True)
        for t in range(TILES):
            nc.vector.memset(neg_g[t][:, 0:PAD], 0.0)
            nc.vector.memset(neg_h[t][:, 0:PAD], 0.0)
            nc.scalar.activation(gate[t][:, 0:PAD], neg_g[t][:, 0:PAD], SIGMOID)

        def load_words(o):
            nc.sync.dma_start(
                out=word_table[o][:].bitcast(I32),
                in_=x_words[o].rearrange("p n r -> p (n r)").bitcast(I32),
            )

        def load_scales(first, last):
            for n in range(first, last):
                r, o = divmod(n, PASSES)
                nc.sync.dma_start(
                    out=scale_table[4 * o + r : P : 32, :].bitcast(I32),
                    in_=x_scales[o, r : 16 : 4, :].bitcast(I32),
                )

        def half(h):
            return slice(h * HALF, (h + 1) * HALF)

        def window(tile, h, back):
            return tile[:, PAD + h * HALF - back : PAD + (h + 1) * HALF - back]

        def load_weight(kind, o, t):
            w = w2 if kind == "gate" else w1
            if (kind, o, t) == ("value", 1, 0):
                flat = rr[0][:]
            else:
                flat = keep.tile([P, PACK * P], F32, name=f"{kind}_raw{o}{t}")[:]
            raw = flat.rearrange("p (j n) -> p j n", j=PACK)
            rows = w[o * P * PACK : (o + 1) * P * PACK, t * P : (t + 1) * P]
            nc.sync.dma_start(out=raw, in_=rows.rearrange("(p j) n -> p j n", j=PACK))
            return raw

        pieces = [(kind, o, t) for t in range(TILES) for kind in ("gate", "value") for o in range(PASSES)]
        raw = {}
        for piece in pieces[:2]:
            raw[piece] = load_weight(*piece)
        load_scales(0, 5)
        load_words(0)
        nc.sync.dma_start(offsets[:], offs)
        load_scales(5, 8)
        load_words(1)
        for piece in pieces[2:]:
            raw[piece] = load_weight(*piece)

        grouped = {}
        shared = []
        quantised = {}

        def cast(kind, o, t, on_vector):
            if (kind, o, t) == ("value", 1, 1):
                tile = far[0][:, half(1)].bitcast(BF16)
            else:
                tile = keep.tile([P, P * PACK], BF16, name=f"{kind}_grouped{o}{t}", align_bytes=64)[:]
            src = raw[kind, o, t].rearrange("p j (c i) -> p c j i", i=4)
            dst = tile.rearrange("p (c i j) -> p c j i", i=4, j=PACK)
            if on_vector:
                nc.vector.tensor_copy(out=dst, in_=src)
            elif (kind, o, t) == pieces[-1]:
                nc.scalar.copy(out=dst[:, :16], in_=src[:, :16])
                shared.append((dst[:, 16:], src[:, 16:]))
            else:
                nc.scalar.copy(out=dst, in_=src)
            grouped[kind, o, t] = tile

        def quantise(kind, o, t):
            if (kind, t) == ("gate", 0):
                codes = first_codes[:, o * P : (o + 1) * P]
                plane = first_planes[:, o * P : (o + 1) * P]
            else:
                codes = keep.tile([P, P], U32, name=f"{kind}_codes{o}{t}", align_bytes=64)[:]
                plane = keep.tile([P, P], U8, name=f"{kind}_plane{o}{t}", align_bytes=64)[:]
            nc.vector.quantize_mx(
                out=codes.bitcast(FP8X4),
                scales=plane,
                in_=grouped[kind, o, t],
            )
            quantised[kind, o, t] = (codes, plane)

        def multiply(kind, o, t, halves=range(HALVES)):
            codes, plane = quantised[kind, o, t]
            for h in halves:
                nc.tensor.matmul_mx(
                    out=banks[kind, t, h][:],
                    lhsT=codes.bitcast(FP8X4),
                    lhsT_scale=plane,
                    rhs=words[o][:, half(h)].bitcast(FP8X4),
                    rhs_scale=scales[4 * o : P, half(h)],
                    start=(o == 0),
                    stop=(o == PASSES - 1),
                )

        def sigmoid(t):
            for h in range(HALVES):
                nc.scalar.activation(window(gate[t], h, 0), banks["gate", t, h][:], SIGMOID)

        def pair_gates(t, h):
            nc.vector.tensor_tensor(rr[t][:, half(h)], window(gate[t], h, 0), window(gate[t], h, 1), ALU.mult)

        def gated_input(t, h):
            nc.vector.scalar_tensor_tensor(
                window(neg_g[t], h, 0), window(gate[t], h, 0), 1.0, banks["value", t, h][:], ALU.subtract, ALU.mult
            )


        def near_term(t, h):
            nc.vector.tensor_tensor(near[t][:, half(h)], window(gate[t], h, 0), window(neg_g[t], h, 1), ALU.mult)

        def first_round(t, h):
            nc.vector.tensor_tensor(window(neg_h[t], h, 0), window(neg_g[t], h, 0), near[t][:, half(h)], ALU.add)

        def far_term(t, h):
            nc.vector.tensor_tensor(far[t][:, half(h)], rr[t][:, half(h)], window(neg_h[t], h, 2), ALU.mult)

        def second_round(t, h):
            pieces_out = 2 if (t, h) == (TILES - 1, HALVES - 1) else 1
            width = HALF // pieces_out
            for n in range(pieces_out):
                cols = slice(h * HALF + n * width, h * HALF + (n + 1) * width)
                nc.vector.scalar_tensor_tensor(
                    result[t][:, cols], neg_h[t][:, PAD : PAD + S][:, cols], -1.0, far[t][:, cols], ALU.mult, ALU.subtract
                )
                nc.sync.dma_start(out=out[t * P : (t + 1) * P, cols], in_=result[t][:, cols])

        turned_banks = {}

        def turn_term(term, t, h, first):
            if first:
                turned_banks[h] = psum.tile([P, HALF], F32, name=f"gate_bank{t}{h}")
            for b in range(HALF // P):
                cols = slice(h * HALF + b * P, h * HALF + (b + 1) * P)
                nc.tensor.matmul(
                    turned_banks[h][:, b * P : (b + 1) * P],
                    term[:, cols],
                    identity[:],
                    start=(first and b == 0),
                    stop=(not first and b == HALF // P - 1),
                    is_transpose=True,
                )

        def second_round_turned(t, h):
            turned_bank = turned_banks[h]
            turn_term(far[t][:], t, h, False)
            turned = keep.tile([P, HALF], F32, name=f"turned{h}")
            nc.scalar.activation(turned[:], turned_bank[:], COPY, scale=-1.0)
            back_bank = psum.tile([P, HALF], F32, name=f"value_bank{t}{h}")
            for b in range(HALF // P):
                nc.tensor.transpose(back_bank[:, b * P : (b + 1) * P], turned[:, b * P : (b + 1) * P], identity[:])
            nc.scalar.copy(out=result[t][:, half(h)], in_=back_bank[:])
            nc.scalar.dma_start(out=out[t * P : (t + 1) * P, half(h)], in_=result[t][:, half(h)])

        steps = (pair_gates, gated_input, near_term, first_round, far_term, second_round)

        nc.vector.tensor_copy(words[0][:], word_table[0][:].indirect(offsets[:]))
        nc.vector.tensor_copy(scales[:], scale_table[:].indirect(offsets[:]))
        for h in range(HALVES):
            part = offsets[:, h * HALF // 16 : (h + 1) * HALF // 16]
            nc.vector.tensor_copy(words[1][:, half(h)], word_table[1][:].indirect(part))

        for kind, o, t in pieces[: 2 * PASSES]:
            cast(kind, o, t, on_vector=(kind == "value" and o == 1))
        for piece in pieces[:PASSES]:
            quantise(*piece)
        warm_codes = keep.tile([P, P], U32, name="warm_codes", tag="scale_table", align_bytes=64)
        nc.scalar.copy(out=warm_codes[:], in_=first_codes[:, 0:P])
        for start, width in ((0, 2 * P), (2 * P, P)):
            nc.tensor.matmul_mx(
                out=warm_bank[:, start : start + width],
                lhsT=warm_codes[:].bitcast(FP8X4),
                lhsT_scale=first_planes[:, 0:P],
                rhs=first_codes[:, 0:width].bitcast(FP8X4),
                rhs_scale=first_planes[:, 0:width],
                start=True,
                stop=True,
            )
        for piece in pieces[:PASSES]:
            multiply(*piece)
        for piece in pieces[PASSES : 2 * PASSES]:
            quantise(*piece)
        for h in range(HALVES):
            for piece in pieces[PASSES : 2 * PASSES]:
                multiply(*piece, [h])
        sigmoid(0)
        later = pieces[2 * PASSES :]
        for piece in later:
            cast(*piece, on_vector=False)
        placed = 0
        for n, step in enumerate(steps[:-1]):
            for h in range(HALVES):
                step(0, h)
                if (n, h) == (3, 0):
                    nc.vector.tensor_copy(out=shared[0][0], in_=shared[0][1])
                if step is first_round:
                    turn_term(neg_h[0][:, PAD : PAD + S], 0, h, True)
                if (n, h) in ((1, 1), (2, 1), (3, 1), (4, 0)):
                    piece = later[placed]
                    placed = placed + 1
                    quantise(*piece)
                    multiply(*piece)
                    if piece == ("gate", PASSES - 1, 1):
                        sigmoid(1)
        for h in range(HALVES):
            second_round_turned(0, h)
        for step in steps:
            for h in range(HALVES):
                step(1, h)
